import numpy as np
import ml_dtypes


def mxq(x, axis, fmt="e4m3"):
    dtype, down = {"e4m3": (ml_dtypes.float8_e4m3fn, 7), "e5m2": (ml_dtypes.float8_e5m2, 14)}[fmt]
    v = np.moveaxis(np.asarray(x, np.float32).astype(ml_dtypes.bfloat16).astype(np.float64), axis, -1)
    blocks = v.reshape(v.shape[:-1] + (-1, 32))
    amax = np.abs(blocks).max(-1, keepdims=True)
    byte = np.maximum(np.where(amax > 0, np.frexp(amax)[1] - 1 + 127, 0) - down, 1)
    scale = np.exp2(byte - 127.0)
    codes = (blocks / scale).astype(np.float32).astype(dtype).astype(np.float64)
    return np.moveaxis((codes * scale).reshape(v.shape), -1, axis)


WIDE = False


def mx_kscale(k):
    if not WIDE:
        return np.ones(k)
    levels = np.array([10, -10, 5, -5, 0])
    if k % 512:
        return np.exp2(np.random.permutation(np.resize(levels, k // 32))).repeat(32)
    a = np.empty((k // 512, 16))
    for p in range(k // 512):
        a[p, :8] = np.random.permutation(np.resize(levels, 8))
        for g in range(8):
            far = levels[np.abs(levels - a[p, g]) >= 10]
            a[p, g + 8] = far[np.random.randint(len(far))]
    return np.exp2(a.ravel()).repeat(32)


BF16 = ml_dtypes.bfloat16


def bf(x):
    return np.asarray(x, np.float32).astype(BF16)


def f64(x):
    return np.asarray(x).astype(np.float64)


E2M1 = np.array([0.0, 0.5, 1.0, 1.5, 2.0, 3.0, 4.0, 6.0, -0.0, -0.5, -1.0, -1.5, -2.0, -3.0, -4.0, -6.0])


def pack_weight(w, fmt):
    k, n = w.shape
    w = f64(bf(w)).reshape(k // 32, 32, n)
    amax = np.abs(w).max(1)
    if fmt == "e4m3":
        byte = np.frexp(amax)[1] - 1 + 127 - 7
    else:
        mant, ex = np.frexp(amax / 6.0)
        byte = np.where(mant > 0.5, ex, ex - 1) + 127
    byte = np.clip(np.where(amax > 0, byte, 1), 1, 254)
    scaled = (w * np.exp2(127.0 - byte)[:, None, :]).reshape(k, n).astype(np.float32)
    by_word = np.ascontiguousarray(scaled.reshape(k // 512, 128, 4, n).transpose(0, 1, 3, 2))
    if fmt == "e4m3":
        words = by_word.astype(ml_dtypes.float8_e4m3fn).view(np.uint8)
    else:
        c = by_word.astype(ml_dtypes.float4_e2m1fn).view(np.uint8) & 0xF
        words = c[..., 0::2] | (c[..., 1::2] << 4)
    return np.ascontiguousarray(words), np.ascontiguousarray(byte.astype(np.uint8).reshape(k // 512, 16, n))


def unpack_weight(words, scales, fmt):
    g, p, n, _ = words.shape
    if fmt == "e4m3":
        vals = np.ascontiguousarray(words).view(ml_dtypes.float8_e4m3fn).astype(np.float64)
    else:
        nib = np.empty((g, p, n, 4), np.uint8)
        nib[..., 0::2] = words & 0xF
        nib[..., 1::2] = words >> 4
        vals = E2M1[nib]
    vals = vals * np.repeat(np.exp2(scales.astype(np.float64) - 127.0), 8, axis=1)[..., None]
    return vals.transpose(0, 1, 3, 2).reshape(g * 512, n)
def pack4(w):
    words, scales = pack_weight(w, "e2m1")
    return words.reshape(words.shape[0], 128, -1), scales


def unpack4(words, scales):
    return unpack_weight(words.reshape(words.shape[0], 128, -1, 2), scales, "e2m1")


M, N = 1536, 1024
C_EYE, C_ZY = 1.5, 0.5


def draw0():
    s, t = mx_kscale(N), mx_kscale(N)
    y = np.eye(N) + np.random.standard_normal((N, N)) / np.sqrt(N)
    zt = np.eye(N) + np.random.standard_normal((N, N)) / np.sqrt(N)
    z_words, z_scales = pack4(zt / s[:, None] / t)
    return {"x": bf(np.random.standard_normal((M, N)) / s),
            "y": bf(y * s[:, None] * t),
            "z_words": z_words,
            "z_scales": z_scales,
            "gain": bf((1 + 0.1 * np.random.standard_normal(N)) / t)}


def core(x, y, z_words, z_scales, gain):
    zt = unpack4(z_words, z_scales)
    yq = mxq(f64(y), 0, "e4m3")
    v = mxq(f64(x), 1, "e4m3") @ yq
    zy = zt.T @ yq
    c = C_EYE * np.eye(N) - C_ZY * zy
    return (mxq(v, 1, "e4m3") @ mxq(c, 0, "e4m3")) * f64(gain)


def e4m3fn_bytes(y):
    return np.clip(np.asarray(y, np.float64), -448.0, 448.0).astype(np.float32).astype(ml_dtypes.float8_e4m3fn).view(np.uint8)


def e4m3fn_values(b):
    return np.asarray(b, np.uint8).view(ml_dtypes.float8_e4m3fn).astype(np.float64)


def setup_inputs():
    d = draw0()
    x0 = np.asarray(d['x']).astype(np.float64)
    s = (np.max(np.abs(x0), axis=(0,), keepdims=True) / 448.0).astype(np.float32)
    out = {}
    for k, v in d.items():
        if k == 'x':
            out['x_bytes'] = e4m3fn_bytes(x0 / s.astype(np.float64))
            out['x_scale'] = s
        else:
            out[k] = v
    return out


def reference(x_bytes, x_scale, y, z_words, z_scales, gain):
    return core(e4m3fn_values(x_bytes) * x_scale.astype(np.float64), y, z_words, z_scales, gain)

@@ -1,0 +1,359 @@
+from contextlib import ExitStack
+
+import concourse.mybir as mybir
+from concourse.masks import make_identity
+
+M, N = 1536, 1024
+FLOPS = 2 * N * N * (2 * M + N)
+
+F32 = mybir.dt.float32
+BF16 = mybir.dt.bfloat16
+I32 = mybir.dt.int32
+U32 = mybir.dt.uint32
+U8 = mybir.dt.uint8
+FP8 = mybir.dt.float8_e4m3fn
+FP8X4 = mybir.dt.float8_e4m3fn_x4
+FP4X4 = mybir.dt.float4_e2m1fn_x4
+MULT = mybir.AluOpType.mult
+ADD = mybir.AluOpType.add
+COPY = mybir.ActivationFunctionType.Copy
+
+P = 128
+TILES = M // P
+PAIRS = TILES // 2
+
+
+def tile_coupled_newton_colouring_step_s11_kernel(tc, x_bytes, x_scale, y, z_words, z_scales, gain, out):
+    nc = tc.nc
+    with ExitStack() as ctx:
+        keep = ctx.enter_context(tc.tile_pool(name="keep", bufs=1))
+        work = ctx.enter_context(tc.tile_pool(name="work", bufs=3))
+        psum = ctx.enter_context(tc.psum_pool(name="psum", bufs=2))
+        ctx.enter_context(tc.manual_schedule())
+
+        xs_col = keep.tile([P, 8], F32, name="xs_col")
+        nc.sync.dma_start(out=xs_col[:], in_=x_scale.rearrange("o (p j) -> p (o j)", j=8))
+        zs_raw = keep.tile([P, 2, N], U8, name="zs_raw", align_bytes=64)
+        nc.vector.memset(zs_raw[:].rearrange("p g n -> p (g n)").bitcast(I32), 0)
+        for q in range(4):
+            nc.sync.dma_start(
+                out=zs_raw[32 * q : 32 * q + 4, :, :].bitcast(I32),
+                in_=z_scales[:, 4 * q : 4 * q + 4, :].bitcast(I32).rearrange("g r n -> r g n"),
+            )
+        y_view = y.rearrange("(g p j) n -> g p j n", p=P, j=4)
+        y_raw = {}
+        zw_raw = keep.tile([P, 2, 2 * N], U8, name="zw_raw", align_bytes=64)
+        xb = []
+
+        def load_y(kp, h):
+            t = keep.tile([P, 4, 512], BF16, name=f"y_raw_{kp}{h}", align_bytes=64)
+            nc.sync.dma_start(out=t[:], in_=y_view[kp][:, :, 512 * h : 512 * h + 512])
+            y_raw[kp, h] = t
+
+        x_view = x_bytes.rearrange("(i s p) k -> i p s k", s=2, p=P)
+
+        def load_x(pair):
+            t = keep.tile([P, 2, N], U8, name=f"xb_{pair}", align_bytes=64)
+            nc.sync.dma_start(out=t[:], in_=x_view[pair])
+            xb.append(t)
+
+        for kp in range(2):
+            nc.sync.dma_start(out=zw_raw[:, kp, :].bitcast(I32), in_=z_words[kp].bitcast(I32))
+        load_y(0, 0)
+        load_y(1, 0)
+        load_x(0)
+        load_y(0, 1)
+        load_y(1, 1)
+        for pair in range(1, PAIRS):
+            load_x(pair)
+        gain_bc = keep.tile([P, N], BF16, name="gain_bc", align_bytes=64)
+        nc.sync.dma_start(out=gain_bc[:], in_=gain.partition_broadcast(P))
+
+        ident = keep.tile([P, P], F32, name="ident", align_bytes=64)
+        make_identity(nc, ident[:])
+        diag = keep.tile([P, 516], F32, name="diag", align_bytes=64)
+        nc.gpsimd.memset(diag[:], 0.0)
+        nc.gpsimd.tensor_scalar(out=diag[:, 3:512:4], in0=ident[:], scalar1=1.5, scalar2=0.0, op0=MULT, op1=ADD)
+
+        xsb = keep.tile([P, N], F32, name="xsb", align_bytes=64)
+        for half in range(2):
+            ps = psum.tile([P, 4, P], F32, name="xt", tag="xt", bufs=2)
+            for j in range(4):
+                nc.tensor.transpose(ps[:, j, :], xs_col[:, 4 * half + j : 4 * half + j + 1].to_broadcast([P, P]), ident[:])
+            nc.scalar.copy(
+                out=xsb[:].rearrange("p (c j) -> p c j", j=8)[:, :, 4 * half : 4 * half + 4],
+                in_=ps[:].rearrange("p j c -> p c j"),
+            )
+
+        yq = keep.tile([P, 2, N], U32, name="yq", align_bytes=64)
+        ys = keep.tile([P, 2, N], U8, name="ys", align_bytes=64)
+        zq = keep.tile([P, 2, 2 * N], U8, name="zq", align_bytes=64)
+        zs = keep.tile([P, 2, N], U8, name="zs", align_bytes=64)
+        cq = keep.tile([P, 2, N], U32, name="cq", align_bytes=64)
+        cs = keep.tile([P, 2, N], U8, name="cs", align_bytes=64)
+        yi = {}
+        ci = {}
+
+        def y_lay(kp, h, t, copy):
+            if (kp, h) not in yi:
+                yi[kp, h] = keep.tile([P, 512, 4], BF16, name=f"yi_{kp}{h}", align_bytes=64)
+            dst = yi[kp, h][:].rearrange("p (t q r) j -> p t q r j", t=4, r=8)
+            raw = y_raw[kp, h][:].rearrange("p j (q t r) -> p t q r j", t=4, r=8)
+            copy(out=dst[:, t], in_=raw[:, t])
+
+        def y_quant(kp, h, t0, nt):
+            lo, hi = 128 * t0, 128 * (t0 + nt)
+            nc.vector.quantize_mx(
+                out=yq[:, kp, 512 * h + lo : 512 * h + hi].bitcast(FP8X4),
+                scales=ys[:, kp, 512 * h + lo : 512 * h + hi],
+                in_=yi[kp, h][:, lo:hi].rearrange("p n j -> p (n j)"),
+            )
+
+        def z_lay():
+            for kp in range(2):
+                nc.vector.tensor_copy(
+                    out=zq[:, kp, :].bitcast(I32).rearrange("p (G t q r) -> p G t q r", G=2, t=4, r=4),
+                    in_=zw_raw[:, kp, :].bitcast(I32).rearrange("p (G q t r) -> p G t q r", G=2, t=4, r=4),
+                )
+                nc.vector.tensor_copy(
+                    out=zs[:, kp, :].bitcast(I32).rearrange("p (G t q r) -> p G t q r", G=2, t=4, r=2),
+                    in_=zs_raw[:, kp, :].bitcast(I32).rearrange("p (G q t r) -> p G t q r", G=2, t=4, r=2),
+                )
+
+        xw, xt, xi, xq, xqs = {}, {}, {}, {}, {}
+
+        def widen(i):
+            if i >= TILES:
+                return
+            xw[i] = work.tile([P, N], BF16, name="xw", tag="xw", bufs=4, align_bytes=64)
+            nc.vector.tensor_tensor(out=xw[i][:], in0=xb[i // 2][:, i % 2, :].bitcast(FP8), in1=xsb[:], op=MULT)
+
+        def turn(i):
+            if i >= TILES:
+                return
+            words = xw[i][:].bitcast(F32)
+            xt[i] = psum.tile([P, 2, 2, P], F32, name="xt", tag="xt", bufs=2)
+            for g in range(2):
+                for u in range(2):
+                    nc.tensor.transpose(xt[i][:, g, u, :], words[:, 256 * g + u : 256 * (g + 1) : 2], ident[:])
+
+        def x_out(i):
+            if i >= TILES:
+                return
+            xi[i] = work.tile([P, 2, P, 4], BF16, name="xi", tag="xi", bufs=3, align_bytes=64)
+            nc.scalar.copy(
+                out=xi[i][:].rearrange("p g m t -> p (g m t)").bitcast(F32).rearrange("p (g m u) -> p g m u", g=2, u=2),
+                in_=xt[i][:].rearrange("p g u m -> p g m u"),
+            )
+
+        def x_quant(i):
+            if i >= TILES:
+                return
+            xq[i] = work.tile([P, 2 * P], U32, name="xq", tag="xq", bufs=4, align_bytes=64)
+            xqs[i] = work.tile([P, 2 * P], U8, name="xqs", tag="xqs", bufs=4, align_bytes=64)
+            nc.vector.quantize_mx(
+                out=xq[i][:].bitcast(FP8X4), scales=xqs[i][:], in_=xi[i][:].rearrange("p g m t -> p (g m t)")
+            )
+
+        zps = {}
+
+        def zy(h, t1, g):
+            ps = psum.tile([P, 4, P], F32, name="mm", tag="mm", bufs=3)
+            cols = slice(512 * h + 128 * t1, 512 * h + 128 * t1 + 128)
+            for t in range(4):
+                c0 = 512 * g + 128 * t
+                for kp in range(2):
+                    nc.tensor.matmul_mx(
+                        out=ps[:, t, :],
+                        lhsT=zq[:, kp, 2 * c0 : 2 * c0 + 256].bitcast(FP4X4),
+                        lhsT_scale=zs[:, kp, c0 : c0 + 128],
+                        rhs=yq[:, kp, cols].bitcast(FP8X4),
+                        rhs_scale=ys[:, kp, cols],
+                        start=(kp == 0),
+                        stop=(kp == 1),
+                    )
+            zps[h, t1, g] = ps
+
+        def c_out(h, t1, g):
+            if (g, h) not in ci:
+                ci[g, h] = keep.tile([P, 512, 4], BF16, name=f"ci_{g}{h}", align_bytes=64)
+            src = zps[h, t1, g][:].rearrange("p f (q r) -> p q r f", r=8)
+            dst = ci[g, h][:].rearrange("p (q t r) f -> p t q r f", t=4, r=8)[:, t1]
+            if g == h:
+                nc.vector.scalar_tensor_tensor(
+                    out=dst,
+                    in0=src,
+                    scalar=-0.5,
+                    in1=diag[:, 3 - t1 : 3 - t1 + 512].rearrange("p (q r f) -> p q r f", r=8, f=4),
+                    op0=MULT,
+                    op1=ADD,
+                )
+            else:
+                nc.scalar.activation(out=dst, in_=src, func=COPY, scale=-0.5)
+
+        def c_quant(g, h):
+            nc.vector.quantize_mx(
+                out=cq[:, g, 512 * h : 512 * h + 512].bitcast(FP8X4),
+                scales=cs[:, g, 512 * h : 512 * h + 512],
+                in_=ci[g, h][:].rearrange("p n f -> p (n f)"),
+            )
+
+        vps, vi, vq, vqs = {}, {}, {}, {}
+
+        def v_mm(i):
+            for g in range(2):
+                ps = psum.tile([P, 4, P], F32, name="mm", tag="mm", bufs=3)
+                for t in range(4):
+                    c0 = 512 * g + 128 * t
+                    for kp in range(2):
+                        nc.tensor.matmul_mx(
+                            out=ps[:, t, :],
+                            lhsT=yq[:, kp, c0 : c0 + 128].bitcast(FP8X4),
+                            lhsT_scale=ys[:, kp, c0 : c0 + 128],
+                            rhs=xq[i][:, P * kp : P * kp + P].bitcast(FP8X4),
+                            rhs_scale=xqs[i][:, P * kp : P * kp + P],
+                            start=(kp == 0),
+                            stop=(kp == 1),
+                        )
+                vps[i, g] = ps
+
+        def v_out(i):
+            vi[i] = work.tile([P, 2, P, 4], BF16, name="vi", tag="vi", bufs=3, align_bytes=64)
+            for g in range(2):
+                nc.scalar.copy(out=vi[i][:, g], in_=vps[i, g][:].rearrange("p t m -> p m t"))
+
+        def v_quant(i):
+            vq[i] = work.tile([P, 2 * P], U32, name="vq", tag="vq", bufs=3, align_bytes=64)
+            vqs[i] = work.tile([P, 2 * P], U8, name="vqs", tag="vqs", bufs=3, align_bytes=64)
+            nc.vector.quantize_mx(
+                out=vq[i][:].bitcast(FP8X4), scales=vqs[i][:], in_=vi[i][:].rearrange("p g m t -> p (g m t)")
+            )
+
+        ops = {}
+
+        def o_mm(i):
+            if i < 0:
+                return
+            for h in range(2):
+                ps = psum.tile([P, 512], F32, name="ops", tag="ops", bufs=3)
+                for g in range(2):
+                    nc.tensor.matmul_mx(
+                        out=ps[:],
+                        lhsT=vq[i][:, P * g : P * g + P].bitcast(FP8X4),
+                        lhsT_scale=vqs[i][:, P * g : P * g + P],
+                        rhs=cq[:, g, 512 * h : 512 * h + 512].bitcast(FP8X4),
+                        rhs_scale=cs[:, g, 512 * h : 512 * h + 512],
+                        start=(g == 0),
+                        stop=(g == 1),
+                    )
+                ops[i, h] = ps
+
+        out_view = out.rearrange("(i p) n -> i p n", p=P)
+
+        def o_out(i):
+            if i < 0:
+                return
+            ot = work.tile([P, N], F32, name="ot", tag="ot", bufs=4, align_bytes=64)
+            for h in range(2):
+                c = slice(512 * h, 512 * h + 512)
+                nc.vector.tensor_tensor(out=ot[:, c], in0=ops[i, h][:], in1=gain_bc[:, c], op=MULT)
+                if i == TILES - 1:
+                    nc.sync.dma_start(out=out_view[i][:, c], in_=ot[:, c])
+            if i < TILES - 1:
+                nc.sync.dma_start(out=out_view[i], in_=ot[:])
+
+        V, S = nc.vector.tensor_copy, nc.scalar.copy
+        z_lay()
+        y_lay(0, 0, 0, V)
+        y_lay(0, 0, 1, S)
+        y_lay(0, 0, 2, S)
+        y_lay(0, 0, 3, V)
+        y_quant(0, 0, 0, 1)
+        y_lay(1, 0, 0, V)
+        y_lay(1, 0, 1, S)
+        y_lay(1, 0, 2, S)
+        y_lay(1, 0, 3, V)
+        y_quant(1, 0, 0, 1)
+        y_quant(0, 0, 1, 1)
+        y_quant(1, 0, 1, 1)
+        zy(0, 0, 0)
+        zy(0, 0, 1)
+        y_quant(0, 0, 2, 2)
+        c_out(0, 0, 0)
+        c_out(0, 0, 1)
+        y_quant(1, 0, 2, 2)
+        y_lay(0, 1, 0, S)
+        y_lay(0, 1, 1, S)
+        zy(0, 1, 0)
+        zy(0, 1, 1)
+        widen(0)
+        c_out(0, 1, 0)
+        c_out(0, 1, 1)
+        y_lay(0, 1, 2, S)
+        y_lay(1, 1, 0, S)
+        zy(0, 2, 0)
+        zy(0, 2, 1)
+        widen(1)
+        c_out(0, 2, 0)
+        c_out(0, 2, 1)
+        y_lay(1, 1, 1, S)
+        y_lay(1, 1, 2, S)
+        zy(0, 3, 0)
+        zy(0, 3, 1)
+        y_lay(0, 1, 3, V)
+        y_lay(1, 1, 3, V)
+        c_out(0, 3, 0)
+        c_out(0, 3, 1)
+        turn(0)
+        turn(1)
+        x_out(0)
+        x_out(1)
+        y_quant(0, 1, 0, 4)
+        y_quant(1, 1, 0, 4)
+        zy(1, 0, 0)
+        zy(1, 0, 1)
+        x_quant(0)
+        x_quant(1)
+        c_out(1, 0, 1)
+        c_out(1, 0, 0)
+        c_quant(0, 0)
+        c_quant(1, 0)
+        zy(1, 1, 0)
+        zy(1, 1, 1)
+        c_out(1, 1, 1)
+        c_out(1, 1, 0)
+        widen(2)
+        zy(1, 2, 0)
+        zy(1, 2, 1)
+        c_out(1, 2, 1)
+        c_out(1, 2, 0)
+        widen(3)
+        zy(1, 3, 0)
+        zy(1, 3, 1)
+        c_out(1, 3, 1)
+        c_out(1, 3, 0)
+        for pair in range(PAIRS):
+            a, b, c, d, e, f = [2 * pair + n for n in range(6)]
+            v_mm(a)
+            v_out(a)
+            if pair == 0:
+                c_quant(0, 1)
+                c_quant(1, 1)
+            widen(e)
+            o_mm(a - 1)
+            v_quant(a)
+            o_out(a - 1)
+            turn(c)
+            turn(d)
+            x_out(c)
+            x_out(d)
+            x_quant(c)
+            x_quant(d)
+            v_mm(b)
+            v_out(b)
+            widen(f)
+            o_mm(a)
+            v_quant(b)
+            o_out(a)
+        o_mm(TILES - 1)
+        o_out(TILES - 1)

@@ -57,30 +57,37 @@ def tile_coupled_newton_colouring_step_s11_kernel(tc, x_bytes, x_scale, y, z_wor
             nc.sync.dma_start(out=t[:], in_=x_view[pair])
             xb.append(t)
 
-        for kp in range(2):
-            nc.sync.dma_start(out=zw_raw[:, kp, :].bitcast(I32), in_=z_words[kp].bitcast(I32))
+        def load_z(g):
+            for kp in range(2):
+                nc.sync.dma_start(
+                    out=zw_raw[:, kp, N * g : N * g + N].bitcast(I32), in_=z_words[kp][:, N * g : N * g + N].bitcast(I32)
+                )
+
+        load_x(0)
+        load_z(0)
         load_y(0, 0)
         load_y(1, 0)
-        load_x(0)
+        load_z(1)
+        load_x(1)
         load_y(0, 1)
         load_y(1, 1)
-        for pair in range(1, PAIRS):
+        for pair in range(2, PAIRS):
             load_x(pair)
         gain_bc = keep.tile([P, N], BF16, name="gain_bc", align_bytes=64)
         nc.sync.dma_start(out=gain_bc[:], in_=gain.partition_broadcast(P))
 
         ident = keep.tile([P, P], F32, name="ident", align_bytes=64)
         make_identity(nc, ident[:])
-        diag = keep.tile([P, 516], F32, name="diag", align_bytes=64)
-        nc.gpsimd.memset(diag[:], 0.0)
-        nc.gpsimd.tensor_scalar(out=diag[:, 3:512:4], in0=ident[:], scalar1=1.5, scalar2=0.0, op0=MULT, op1=ADD)
+        eye15 = keep.tile([P, P], F32, name="eye15", align_bytes=64)
+        nc.gpsimd.tensor_scalar(out=eye15[:], in0=ident[:], scalar1=1.5, scalar2=0.0, op0=MULT, op1=ADD)
 
         xsb = keep.tile([P, N], F32, name="xsb", align_bytes=64)
         for half in range(2):
             ps = psum.tile([P, 4, P], F32, name="xt", tag="xt", bufs=2)
             for j in range(4):
                 nc.tensor.transpose(ps[:, j, :], xs_col[:, 4 * half + j : 4 * half + j + 1].to_broadcast([P, P]), ident[:])
-            nc.scalar.copy(
+            copy = nc.vector.tensor_copy if half else nc.scalar.copy
+            copy(
                 out=xsb[:].rearrange("p (c j) -> p c j", j=8)[:, :, 4 * half : 4 * half + 4],
                 in_=ps[:].rearrange("p j c -> p c j"),
             )
@@ -109,15 +116,15 @@ def tile_coupled_newton_colouring_step_s11_kernel(tc, x_bytes, x_scale, y, z_wor
                 in_=yi[kp, h][:, lo:hi].rearrange("p n j -> p (n j)"),
             )
 
-        def z_lay():
+        def z_lay(g):
             for kp in range(2):
                 nc.vector.tensor_copy(
-                    out=zq[:, kp, :].bitcast(I32).rearrange("p (G t q r) -> p G t q r", G=2, t=4, r=4),
-                    in_=zw_raw[:, kp, :].bitcast(I32).rearrange("p (G q t r) -> p G t q r", G=2, t=4, r=4),
+                    out=zq[:, kp, N * g : N * g + N].bitcast(I32).rearrange("p (t q r) -> p t q r", t=4, r=4),
+                    in_=zw_raw[:, kp, N * g : N * g + N].bitcast(I32).rearrange("p (q t r) -> p t q r", t=4, r=4),
                 )
                 nc.vector.tensor_copy(
-                    out=zs[:, kp, :].bitcast(I32).rearrange("p (G t q r) -> p G t q r", G=2, t=4, r=2),
-                    in_=zs_raw[:, kp, :].bitcast(I32).rearrange("p (G q t r) -> p G t q r", G=2, t=4, r=2),
+                    out=zs[:, kp, 512 * g : 512 * g + 512].bitcast(I32).rearrange("p (t q r) -> p t q r", t=4, r=2),
+                    in_=zs_raw[:, kp, 512 * g : 512 * g + 512].bitcast(I32).rearrange("p (q t r) -> p t q r", t=4, r=2),
                 )
 
         xw, xt, xi, xq, xqs = {}, {}, {}, {}, {}
@@ -125,22 +132,31 @@ def tile_coupled_newton_colouring_step_s11_kernel(tc, x_bytes, x_scale, y, z_wor
         def widen(i):
             if i >= TILES:
                 return
-            xw[i] = work.tile([P, N], BF16, name="xw", tag="xw", bufs=4, align_bytes=64)
+            xw[i] = work.tile([P, N], BF16, name="xw", tag="xw", bufs=6, align_bytes=64)
             nc.vector.tensor_tensor(out=xw[i][:], in0=xb[i // 2][:, i % 2, :].bitcast(FP8), in1=xsb[:], op=MULT)
+
+        xp = {}
+
+        def x_perm(i):
+            if i >= TILES:
+                return
+            xp[i] = work.tile([P, 2, 2, P], F32, name="xp", tag="xp", bufs=6, align_bytes=64)
+            nc.scalar.copy(out=xp[i][:], in_=xw[i][:].bitcast(F32).rearrange("p (g n u) -> p g u n", g=2, u=2))
 
         def turn(i):
             if i >= TILES:
                 return
-            words = xw[i][:].bitcast(F32)
+            perm = i in xp
+            words = xp[i][:].rearrange("p g u n -> p (g u n)") if perm else xw[i][:].bitcast(F32)
             xt[i] = psum.tile([P, 2, 2, P], F32, name="xt", tag="xt", bufs=2)
             for g in range(2):
                 for u in range(2):
-                    nc.tensor.transpose(xt[i][:, g, u, :], words[:, 256 * g + u : 256 * (g + 1) : 2], ident[:])
+                    nc.tensor.transpose(xt[i][:, g, u, :], words[:, 256 * g + 128 * u : 256 * g + 128 * u + 128] if perm else words[:, 256 * g + u : 256 * (g + 1) : 2], ident[:])
 
         def x_out(i):
             if i >= TILES:
                 return
-            xi[i] = work.tile([P, 2, P, 4], BF16, name="xi", tag="xi", bufs=3, align_bytes=64)
+            xi[i] = work.tile([P, 2, P, 4], BF16, name="xi", tag="xi", bufs=4, align_bytes=64)
             nc.scalar.copy(
                 out=xi[i][:].rearrange("p g m t -> p (g m t)").bitcast(F32).rearrange("p (g m u) -> p g m u", g=2, u=2),
                 in_=xt[i][:].rearrange("p g u m -> p g m u"),
@@ -149,8 +165,8 @@ def tile_coupled_newton_colouring_step_s11_kernel(tc, x_bytes, x_scale, y, z_wor
         def x_quant(i):
             if i >= TILES:
                 return
-            xq[i] = work.tile([P, 2 * P], U32, name="xq", tag="xq", bufs=4, align_bytes=64)
-            xqs[i] = work.tile([P, 2 * P], U8, name="xqs", tag="xqs", bufs=4, align_bytes=64)
+            xq[i] = work.tile([P, 2 * P], U32, name="xq", tag="xq", bufs=6, align_bytes=64)
+            xqs[i] = work.tile([P, 2 * P], U8, name="xqs", tag="xqs", bufs=6, align_bytes=64)
             nc.vector.quantize_mx(
                 out=xq[i][:].bitcast(FP8X4), scales=xqs[i][:], in_=xi[i][:].rearrange("p g m t -> p (g m t)")
             )
@@ -174,20 +190,28 @@ def tile_coupled_newton_colouring_step_s11_kernel(tc, x_bytes, x_scale, y, z_wor
                     )
             zps[h, t1, g] = ps
 
-        def c_out(h, t1, g):
+        dblk = {}
+
+        def d_out(h, t1, g):
+            dblk[h, t1] = work.tile([P, P], F32, name="dblk", tag="dblk", bufs=8, align_bytes=64)
+            nc.scalar.activation(out=dblk[h, t1][:], in_=zps[h, t1, g][:, t1, :], func=COPY, scale=-0.5)
+
+        def d_add(h, t1, g):
+            dst = ci[g, h][:].rearrange("p (q t r) f -> p t q r f", t=4, r=8)[:, t1, :, :, t1]
+            nc.gpsimd.tensor_tensor(
+                out=dst,
+                in0=dblk[h, t1][:].rearrange("p (q r) -> p q r", r=8),
+                in1=eye15[:].rearrange("p (q r) -> p q r", r=8),
+                op=ADD,
+            )
+
+        def c_out(h, t1, g, eng):
             if (g, h) not in ci:
                 ci[g, h] = keep.tile([P, 512, 4], BF16, name=f"ci_{g}{h}", align_bytes=64)
             src = zps[h, t1, g][:].rearrange("p f (q r) -> p q r f", r=8)
             dst = ci[g, h][:].rearrange("p (q t r) f -> p t q r f", t=4, r=8)[:, t1]
-            if g == h:
-                nc.vector.scalar_tensor_tensor(
-                    out=dst,
-                    in0=src,
-                    scalar=-0.5,
-                    in1=diag[:, 3 - t1 : 3 - t1 + 512].rearrange("p (q r f) -> p q r f", r=8, f=4),
-                    op0=MULT,
-                    op1=ADD,
-                )
+            if eng == "V":
+                nc.vector.tensor_scalar(out=dst, in0=src, scalar1=-0.5, scalar2=None, op0=MULT)
             else:
                 nc.scalar.activation(out=dst, in_=src, func=COPY, scale=-0.5)
 
@@ -200,8 +224,8 @@ def tile_coupled_newton_colouring_step_s11_kernel(tc, x_bytes, x_scale, y, z_wor
 
         vps, vi, vq, vqs = {}, {}, {}, {}
 
-        def v_mm(i):
-            for g in range(2):
+        def v_mm(i, gs=(0, 1)):
+            for g in gs:
                 ps = psum.tile([P, 4, P], F32, name="mm", tag="mm", bufs=3)
                 for t in range(4):
                     c0 = 512 * g + 128 * t
@@ -217,24 +241,27 @@ def tile_coupled_newton_colouring_step_s11_kernel(tc, x_bytes, x_scale, y, z_wor
                         )
                 vps[i, g] = ps
 
-        def v_out(i):
-            vi[i] = work.tile([P, 2, P, 4], BF16, name="vi", tag="vi", bufs=3, align_bytes=64)
-            for g in range(2):
+        def v_out(i, gs=(0, 1)):
+            if i not in vi:
+                vi[i] = work.tile([P, 2, P, 4], BF16, name="vi", tag="vi", bufs=4, align_bytes=64)
+            for g in gs:
                 nc.scalar.copy(out=vi[i][:, g], in_=vps[i, g][:].rearrange("p t m -> p m t"))
 
         def v_quant(i):
             vq[i] = work.tile([P, 2 * P], U32, name="vq", tag="vq", bufs=3, align_bytes=64)
             vqs[i] = work.tile([P, 2 * P], U8, name="vqs", tag="vqs", bufs=3, align_bytes=64)
-            nc.vector.quantize_mx(
-                out=vq[i][:].bitcast(FP8X4), scales=vqs[i][:], in_=vi[i][:].rearrange("p g m t -> p (g m t)")
-            )
+            parts = [(0, 1), (1, 2)] if i == TILES - 1 else [(0, 2)]
+            for g0, g1 in parts:
+                nc.vector.quantize_mx(
+                    out=vq[i][:, P * g0 : P * g1].bitcast(FP8X4),
+                    scales=vqs[i][:, P * g0 : P * g1],
+                    in_=vi[i][:, g0:g1].rearrange("p g m t -> p (g m t)"),
+                )
 
         ops = {}
 
-        def o_mm(i):
-            if i < 0:
-                return
-            for h in range(2):
+        def o_mm(i, hs=(0, 1)):
+            for h in hs:
                 ps = psum.tile([P, 512], F32, name="ops", tag="ops", bufs=3)
                 for g in range(2):
                     nc.tensor.matmul_mx(
@@ -250,110 +277,263 @@ def tile_coupled_newton_colouring_step_s11_kernel(tc, x_bytes, x_scale, y, z_wor
 
         out_view = out.rearrange("(i p) n -> i p n", p=P)
 
-        def o_out(i):
-            if i < 0:
-                return
-            ot = work.tile([P, N], F32, name="ot", tag="ot", bufs=4, align_bytes=64)
-            for h in range(2):
-                c = slice(512 * h, 512 * h + 512)
-                nc.vector.tensor_tensor(out=ot[:, c], in0=ops[i, h][:], in1=gain_bc[:, c], op=MULT)
-                if i == TILES - 1:
-                    nc.sync.dma_start(out=out_view[i][:, c], in_=ot[:, c])
-            if i < TILES - 1:
-                nc.sync.dma_start(out=out_view[i], in_=ot[:])
+        ot = {}
+
+        def o_out(i, hs=(0, 1)):
+            if i not in ot:
+                ot[i] = work.tile([P, N], F32, name="ot", tag="ot", bufs=4, align_bytes=64)
+            width = 256 if i == TILES - 1 else 512
+            for h in hs:
+                for c0 in range(0, 512, width):
+                    c = slice(512 * h + c0, 512 * h + c0 + width)
+                    nc.vector.tensor_tensor(out=ot[i][:, c], in0=ops[i, h][:, c0 : c0 + width], in1=gain_bc[:, c], op=MULT)
+                    if i == TILES - 1:
+                        nc.sync.dma_start(out=out_view[i][:, c], in_=ot[i][:, c])
+                if h == 1 and i < TILES - 1:
+                    nc.sync.dma_start(out=out_view[i], in_=ot[i][:])
 
         V, S = nc.vector.tensor_copy, nc.scalar.copy
-        z_lay()
-        y_lay(0, 0, 0, V)
-        y_lay(0, 0, 1, S)
-        y_lay(0, 0, 2, S)
-        y_lay(0, 0, 3, V)
-        y_quant(0, 0, 0, 1)
+        widen(1)
+        widen(0)
+        y_lay(0, 0, 3, S)
+        y_lay(0, 0, 1, V)
+        z_lay(0)
+        turn(1)
+        y_lay(0, 0, 0, S)
+        turn(0)
         y_lay(1, 0, 0, V)
-        y_lay(1, 0, 1, S)
-        y_lay(1, 0, 2, S)
-        y_lay(1, 0, 3, V)
+        y_lay(1, 0, 1, V)
+        y_lay(0, 0, 2, V)
+        y_lay(1, 0, 3, S)
         y_quant(1, 0, 0, 1)
-        y_quant(0, 0, 1, 1)
+        y_quant(0, 0, 0, 1)
+        x_out(1)
         y_quant(1, 0, 1, 1)
         zy(0, 0, 0)
-        zy(0, 0, 1)
-        y_quant(0, 0, 2, 2)
-        c_out(0, 0, 0)
-        c_out(0, 0, 1)
-        y_quant(1, 0, 2, 2)
-        y_lay(0, 1, 0, S)
-        y_lay(0, 1, 1, S)
-        zy(0, 1, 0)
-        zy(0, 1, 1)
-        widen(0)
-        c_out(0, 1, 0)
-        c_out(0, 1, 1)
-        y_lay(0, 1, 2, S)
-        y_lay(1, 1, 0, S)
-        zy(0, 2, 0)
-        zy(0, 2, 1)
-        widen(1)
-        c_out(0, 2, 0)
-        c_out(0, 2, 1)
-        y_lay(1, 1, 1, S)
-        y_lay(1, 1, 2, S)
-        zy(0, 3, 0)
-        zy(0, 3, 1)
-        y_lay(0, 1, 3, V)
-        y_lay(1, 1, 3, V)
-        c_out(0, 3, 0)
-        c_out(0, 3, 1)
-        turn(0)
-        turn(1)
+        y_lay(1, 0, 2, S)
+        y_quant(0, 0, 1, 1)
         x_out(0)
-        x_out(1)
-        y_quant(0, 1, 0, 4)
-        y_quant(1, 1, 0, 4)
-        zy(1, 0, 0)
-        zy(1, 0, 1)
+        z_lay(1)
+        y_quant(1, 0, 2, 2)
+        zy(0, 1, 0)
+        y_lay(0, 1, 0, V)
+        d_out(0, 0, 0)
+        zy(0, 1, 1)
         x_quant(0)
+        c_out(0, 0, 0, "S")
+        d_out(0, 1, 0)
+        c_out(0, 1, 0, "S")
+        zy(0, 0, 1)
+        y_lay(1, 1, 1, V)
+        c_out(0, 1, 1, "S")
+        y_quant(0, 0, 2, 2)
+        y_lay(0, 1, 3, V)
         x_quant(1)
-        c_out(1, 0, 1)
-        c_out(1, 0, 0)
-        c_quant(0, 0)
-        c_quant(1, 0)
-        zy(1, 1, 0)
-        zy(1, 1, 1)
-        c_out(1, 1, 1)
-        c_out(1, 1, 0)
+        zy(0, 3, 0)
+        y_lay(1, 1, 3, S)
+        c_out(0, 0, 1, "S")
+        zy(0, 2, 1)
+        y_lay(0, 1, 2, V)
         widen(2)
-        zy(1, 2, 0)
-        zy(1, 2, 1)
-        c_out(1, 2, 1)
-        c_out(1, 2, 0)
-        widen(3)
+        d_out(0, 3, 0)
+        c_out(0, 3, 0, "S")
+        y_lay(0, 1, 1, V)
+        c_out(0, 2, 1, "S")
+        y_lay(1, 1, 0, V)
+        zy(0, 2, 0)
+        y_lay(1, 1, 2, V)
+        d_out(0, 2, 0)
+        v_mm(0, (0,))
+        y_quant(0, 1, 0, 4)
+        c_out(0, 2, 0, "S")
+        v_mm(1, (0,))
+        v_out(0, (0,))
+        v_out(1, (0,))
+        zy(0, 3, 1)
+        y_quant(1, 1, 0, 4)
+        x_perm(2)
         zy(1, 3, 0)
+        c_out(1, 3, 0, "S")
+        c_out(0, 3, 1, "V")
+        zy(1, 0, 1)
+        d_add(0, 1, 0)
+        d_add(0, 0, 0)
+        d_out(1, 0, 1)
+        widen(3)
+        c_out(1, 0, 1, "S")
+        c_quant(1, 0)
+        v_mm(0, (1,))
+        d_add(0, 2, 0)
+        v_out(0, (1,))
+        zy(1, 1, 0)
+        x_perm(3)
+        zy(1, 0, 0)
+        zy(1, 2, 0)
+        c_out(1, 1, 0, "V")
+        turn(2)
+        d_add(0, 3, 0)
+        c_out(1, 0, 0, "S")
+        turn(3)
+        c_out(1, 2, 0, "S")
+        v_mm(1, (1,))
+        v_quant(0)
+        c_quant(0, 0)
+        widen(4)
+        c_quant(0, 1)
+        x_out(2)
+        zy(1, 2, 1)
+        v_out(1, (1,))
+        zy(1, 1, 1)
+        widen(5)
+        d_out(1, 2, 1)
+        v_quant(1)
         zy(1, 3, 1)
-        c_out(1, 3, 1)
-        c_out(1, 3, 0)
-        for pair in range(PAIRS):
-            a, b, c, d, e, f = [2 * pair + n for n in range(6)]
-            v_mm(a)
-            v_out(a)
-            if pair == 0:
-                c_quant(0, 1)
-                c_quant(1, 1)
-            widen(e)
-            o_mm(a - 1)
-            v_quant(a)
-            o_out(a - 1)
-            turn(c)
-            turn(d)
-            x_out(c)
-            x_out(d)
-            x_quant(c)
-            x_quant(d)
-            v_mm(b)
-            v_out(b)
-            widen(f)
-            o_mm(a)
-            v_quant(b)
-            o_out(a)
-        o_mm(TILES - 1)
-        o_out(TILES - 1)
+        x_quant(2)
+        x_out(3)
+        o_mm(0, (0,))
+        c_out(1, 2, 1, "S")
+        o_mm(1, (0,))
+        d_out(1, 1, 1)
+        d_add(1, 2, 1)
+        c_out(1, 1, 1, "V")
+        d_out(1, 3, 1)
+        v_mm(2, (1,))
+        c_out(1, 3, 1, "S")
+        v_mm(2, (0,))
+        o_out(0, (0,))
+        d_add(1, 0, 1)
+        o_out(1, (0,))
+        d_add(1, 1, 1)
+        d_add(1, 3, 1)
+        x_perm(5)
+        x_perm(4)
+        v_out(2, (0,))
+        x_quant(3)
+        c_quant(1, 1)
+        turn(5)
+        turn(4)
+        widen(6)
+        v_out(2, (1,))
+        x_out(5)
+        x_out(4)
+        o_mm(1, (1,))
+        v_quant(2)
+        o_out(1, (1,))
+        o_mm(0, (1,))
+        x_perm(6)
+        x_quant(5)
+        o_out(0, (1,))
+        x_quant(4)
+        v_mm(3, (0,))
+        v_mm(3, (1,))
+        v_out(3, (0,))
+        v_out(3, (1,))
+        widen(7)
+        o_mm(2, (0,))
+        o_mm(2, (1,))
+        v_quant(3)
+        x_perm(7)
+        o_out(2, (0,))
+        o_out(2, (1,))
+        v_mm(4, (0,))
+        v_mm(4, (1,))
+        v_out(4, (0,))
+        v_out(4, (1,))
+        widen(8)
+        o_mm(3, (0,))
+        o_mm(3, (1,))
+        v_quant(4)
+        o_out(3, (0,))
+        o_out(3, (1,))
+        turn(6)
+        turn(7)
+        x_out(6)
+        x_out(7)
+        x_perm(8)
+        x_quant(6)
+        x_quant(7)
+        v_mm(5, (0,))
+        v_mm(5, (1,))
+        v_out(5, (0,))
+        v_out(5, (1,))
+        widen(9)
+        o_mm(4, (0,))
+        o_mm(4, (1,))
+        v_quant(5)
+        x_perm(9)
+        o_out(4, (0,))
+        o_out(4, (1,))
+        v_mm(6, (0,))
+        v_mm(6, (1,))
+        v_out(6, (0,))
+        v_out(6, (1,))
+        widen(10)
+        o_mm(5, (0,))
+        o_mm(5, (1,))
+        v_quant(6)
+        o_out(5, (0,))
+        o_out(5, (1,))
+        turn(8)
+        turn(9)
+        x_out(8)
+        x_out(9)
+        x_perm(10)
+        x_quant(8)
+        x_quant(9)
+        v_mm(7, (0,))
+        v_mm(7, (1,))
+        v_out(7, (0,))
+        v_out(7, (1,))
+        widen(11)
+        o_mm(6, (0,))
+        o_mm(6, (1,))
+        v_quant(7)
+        x_perm(11)
+        o_out(6, (0,))
+        o_out(6, (1,))
+        v_mm(8, (0,))
+        v_mm(8, (1,))
+        v_out(8, (0,))
+        v_out(8, (1,))
+        o_mm(7, (0,))
+        o_mm(7, (1,))
+        v_quant(8)
+        o_out(7, (0,))
+        o_out(7, (1,))
+        turn(10)
+        turn(11)
+        x_out(10)
+        x_out(11)
+        x_quant(10)
+        x_quant(11)
+        v_mm(9, (0,))
+        v_mm(9, (1,))
+        v_out(9, (0,))
+        v_out(9, (1,))
+        o_mm(8, (0,))
+        o_mm(8, (1,))
+        v_quant(9)
+        o_out(8, (0,))
+        o_out(8, (1,))
+        v_mm(10, (0,))
+        v_mm(10, (1,))
+        v_out(10, (0,))
+        v_out(10, (1,))
+        o_mm(9, (0,))
+        o_mm(9, (1,))
+        v_quant(10)
+        o_out(9, (0,))
+        o_out(9, (1,))
+        v_mm(11, (0,))
+        v_mm(11, (1,))
+        v_out(11, (0,))
+        v_out(11, (1,))
+        o_mm(10, (0,))
+        o_mm(10, (1,))
+        v_quant(11)
+        o_out(10, (0,))
+        o_out(10, (1,))
+        o_mm(11, (0,))
+        o_mm(11, (1,))
+        o_out(11, (0,))
+        o_out(11, (1,))

from contextlib import ExitStack

import concourse.mybir as mybir
from concourse.masks import make_identity

M, N = 1536, 1024
FLOPS = 2 * N * N * (2 * M + N)

F32 = mybir.dt.float32
BF16 = mybir.dt.bfloat16
I32 = mybir.dt.int32
U32 = mybir.dt.uint32
U8 = mybir.dt.uint8
FP8 = mybir.dt.float8_e4m3fn
FP8X4 = mybir.dt.float8_e4m3fn_x4
FP4X4 = mybir.dt.float4_e2m1fn_x4
MULT = mybir.AluOpType.mult
ADD = mybir.AluOpType.add
COPY = mybir.ActivationFunctionType.Copy

P = 128
TILES = M // P
PAIRS = TILES // 2


def tile_coupled_newton_colouring_step_s11_kernel(tc, x_bytes, x_scale, y, z_words, z_scales, gain, out):
    nc = tc.nc
    with ExitStack() as ctx:
        keep = ctx.enter_context(tc.tile_pool(name="keep", bufs=1))
        work = ctx.enter_context(tc.tile_pool(name="work", bufs=3))
        psum = ctx.enter_context(tc.psum_pool(name="psum", bufs=2))
        ctx.enter_context(tc.manual_schedule())

        xs_col = keep.tile([P, 8], F32, name="xs_col")
        nc.sync.dma_start(out=xs_col[:], in_=x_scale.rearrange("o (p j) -> p (o j)", j=8))
        zs_raw = keep.tile([P, 2, N], U8, name="zs_raw", align_bytes=64)
        nc.vector.memset(zs_raw[:].rearrange("p g n -> p (g n)").bitcast(I32), 0)
        for q in range(4):
            nc.sync.dma_start(
                out=zs_raw[32 * q : 32 * q + 4, :, :].bitcast(I32),
                in_=z_scales[:, 4 * q : 4 * q + 4, :].bitcast(I32).rearrange("g r n -> r g n"),
            )
        y_view = y.rearrange("(g p j) n -> g p j n", p=P, j=4)
        y_raw = {}
        zw_raw = keep.tile([P, 2, 2 * N], U8, name="zw_raw", align_bytes=64)
        xb = []

        def load_y(kp, h):
            t = keep.tile([P, 4, 512], BF16, name=f"y_raw_{kp}{h}", align_bytes=64)
            nc.sync.dma_start(out=t[:], in_=y_view[kp][:, :, 512 * h : 512 * h + 512])
            y_raw[kp, h] = t

        x_view = x_bytes.rearrange("(i s p) k -> i p s k", s=2, p=P)

        def load_x(pair):
            t = keep.tile([P, 2, N], U8, name=f"xb_{pair}", align_bytes=64)
            nc.sync.dma_start(out=t[:], in_=x_view[pair])
            xb.append(t)

        def load_z(g):
            for kp in range(2):
                nc.sync.dma_start(
                    out=zw_raw[:, kp, N * g : N * g + N].bitcast(I32), in_=z_words[kp][:, N * g : N * g + N].bitcast(I32)
                )

        load_x(0)
        load_z(0)
        load_y(0, 0)
        load_y(1, 0)
        load_z(1)
        load_x(1)
        load_y(0, 1)
        load_y(1, 1)
        for pair in range(2, PAIRS):
            load_x(pair)
        gain_bc = keep.tile([P, N], BF16, name="gain_bc", align_bytes=64)
        nc.sync.dma_start(out=gain_bc[:], in_=gain.partition_broadcast(P))

        ident = keep.tile([P, P], F32, name="ident", align_bytes=64)
        make_identity(nc, ident[:])
        eye15 = keep.tile([P, P], F32, name="eye15", align_bytes=64)
        nc.gpsimd.tensor_scalar(out=eye15[:], in0=ident[:], scalar1=1.5, scalar2=0.0, op0=MULT, op1=ADD)

        xsb = keep.tile([P, N], F32, name="xsb", align_bytes=64)
        for half in range(2):
            ps = psum.tile([P, 4, P], F32, name="xt", tag="xt", bufs=2)
            for j in range(4):
                nc.tensor.transpose(ps[:, j, :], xs_col[:, 4 * half + j : 4 * half + j + 1].to_broadcast([P, P]), ident[:])
            copy = nc.vector.tensor_copy if half else nc.scalar.copy
            copy(
                out=xsb[:].rearrange("p (c j) -> p c j", j=8)[:, :, 4 * half : 4 * half + 4],
                in_=ps[:].rearrange("p j c -> p c j"),
            )

        yq = keep.tile([P, 2, N], U32, name="yq", align_bytes=64)
        ys = keep.tile([P, 2, N], U8, name="ys", align_bytes=64)
        zq = keep.tile([P, 2, 2 * N], U8, name="zq", align_bytes=64)
        zs = keep.tile([P, 2, N], U8, name="zs", align_bytes=64)
        cq = keep.tile([P, 2, N], U32, name="cq", align_bytes=64)
        cs = keep.tile([P, 2, N], U8, name="cs", align_bytes=64)
        yi = {}
        ci = {}

        def y_lay(kp, h, t, copy):
            if (kp, h) not in yi:
                yi[kp, h] = keep.tile([P, 512, 4], BF16, name=f"yi_{kp}{h}", align_bytes=64)
            dst = yi[kp, h][:].rearrange("p (t q r) j -> p t q r j", t=4, r=8)
            raw = y_raw[kp, h][:].rearrange("p j (q t r) -> p t q r j", t=4, r=8)
            copy(out=dst[:, t], in_=raw[:, t])

        def y_quant(kp, h, t0, nt):
            lo, hi = 128 * t0, 128 * (t0 + nt)
            nc.vector.quantize_mx(
                out=yq[:, kp, 512 * h + lo : 512 * h + hi].bitcast(FP8X4),
                scales=ys[:, kp, 512 * h + lo : 512 * h + hi],
                in_=yi[kp, h][:, lo:hi].rearrange("p n j -> p (n j)"),
            )

        def z_lay(g):
            for kp in range(2):
                nc.vector.tensor_copy(
                    out=zq[:, kp, N * g : N * g + N].bitcast(I32).rearrange("p (t q r) -> p t q r", t=4, r=4),
                    in_=zw_raw[:, kp, N * g : N * g + N].bitcast(I32).rearrange("p (q t r) -> p t q r", t=4, r=4),
                )
                nc.vector.tensor_copy(
                    out=zs[:, kp, 512 * g : 512 * g + 512].bitcast(I32).rearrange("p (t q r) -> p t q r", t=4, r=2),
                    in_=zs_raw[:, kp, 512 * g : 512 * g + 512].bitcast(I32).rearrange("p (q t r) -> p t q r", t=4, r=2),
                )

        xw, xt, xi, xq, xqs = {}, {}, {}, {}, {}

        def widen(i):
            if i >= TILES:
                return
            xw[i] = work.tile([P, N], BF16, name="xw", tag="xw", bufs=6, align_bytes=64)
            nc.vector.tensor_tensor(out=xw[i][:], in0=xb[i // 2][:, i % 2, :].bitcast(FP8), in1=xsb[:], op=MULT)

        xp = {}

        def x_perm(i):
            if i >= TILES:
                return
            xp[i] = work.tile([P, 2, 2, P], F32, name="xp", tag="xp", bufs=6, align_bytes=64)
            nc.scalar.copy(out=xp[i][:], in_=xw[i][:].bitcast(F32).rearrange("p (g n u) -> p g u n", g=2, u=2))

        def turn(i):
            if i >= TILES:
                return
            perm = i in xp
            words = xp[i][:].rearrange("p g u n -> p (g u n)") if perm else xw[i][:].bitcast(F32)
            xt[i] = psum.tile([P, 2, 2, P], F32, name="xt", tag="xt", bufs=2)
            for g in range(2):
                for u in range(2):
                    nc.tensor.transpose(xt[i][:, g, u, :], words[:, 256 * g + 128 * u : 256 * g + 128 * u + 128] if perm else words[:, 256 * g + u : 256 * (g + 1) : 2], ident[:])

        def x_out(i):
            if i >= TILES:
                return
            xi[i] = work.tile([P, 2, P, 4], BF16, name="xi", tag="xi", bufs=4, align_bytes=64)
            nc.scalar.copy(
                out=xi[i][:].rearrange("p g m t -> p (g m t)").bitcast(F32).rearrange("p (g m u) -> p g m u", g=2, u=2),
                in_=xt[i][:].rearrange("p g u m -> p g m u"),
            )

        def x_quant(i):
            if i >= TILES:
                return
            xq[i] = work.tile([P, 2 * P], U32, name="xq", tag="xq", bufs=6, align_bytes=64)
            xqs[i] = work.tile([P, 2 * P], U8, name="xqs", tag="xqs", bufs=6, align_bytes=64)
            nc.vector.quantize_mx(
                out=xq[i][:].bitcast(FP8X4), scales=xqs[i][:], in_=xi[i][:].rearrange("p g m t -> p (g m t)")
            )

        zps = {}

        def zy(h, t1, g):
            ps = psum.tile([P, 4, P], F32, name="mm", tag="mm", bufs=3)
            cols = slice(512 * h + 128 * t1, 512 * h + 128 * t1 + 128)
            for t in range(4):
                c0 = 512 * g + 128 * t
                for kp in range(2):
                    nc.tensor.matmul_mx(
                        out=ps[:, t, :],
                        lhsT=zq[:, kp, 2 * c0 : 2 * c0 + 256].bitcast(FP4X4),
                        lhsT_scale=zs[:, kp, c0 : c0 + 128],
                        rhs=yq[:, kp, cols].bitcast(FP8X4),
                        rhs_scale=ys[:, kp, cols],
                        start=(kp == 0),
                        stop=(kp == 1),
                    )
            zps[h, t1, g] = ps

        dblk = {}

        def d_out(h, t1, g):
            dblk[h, t1] = work.tile([P, P], F32, name="dblk", tag="dblk", bufs=8, align_bytes=64)
            nc.scalar.activation(out=dblk[h, t1][:], in_=zps[h, t1, g][:, t1, :], func=COPY, scale=-0.5)

        def d_add(h, t1, g):
            dst = ci[g, h][:].rearrange("p (q t r) f -> p t q r f", t=4, r=8)[:, t1, :, :, t1]
            nc.gpsimd.tensor_tensor(
                out=dst,
                in0=dblk[h, t1][:].rearrange("p (q r) -> p q r", r=8),
                in1=eye15[:].rearrange("p (q r) -> p q r", r=8),
                op=ADD,
            )

        def c_out(h, t1, g, eng):
            if (g, h) not in ci:
                ci[g, h] = keep.tile([P, 512, 4], BF16, name=f"ci_{g}{h}", align_bytes=64)
            src = zps[h, t1, g][:].rearrange("p f (q r) -> p q r f", r=8)
            dst = ci[g, h][:].rearrange("p (q t r) f -> p t q r f", t=4, r=8)[:, t1]
            if eng == "V":
                nc.vector.tensor_scalar(out=dst, in0=src, scalar1=-0.5, scalar2=None, op0=MULT)
            else:
                nc.scalar.activation(out=dst, in_=src, func=COPY, scale=-0.5)

        def c_quant(g, h):
            nc.vector.quantize_mx(
                out=cq[:, g, 512 * h : 512 * h + 512].bitcast(FP8X4),
                scales=cs[:, g, 512 * h : 512 * h + 512],
                in_=ci[g, h][:].rearrange("p n f -> p (n f)"),
            )

        vps, vi, vq, vqs = {}, {}, {}, {}

        def v_mm(i, gs=(0, 1)):
            for g in gs:
                ps = psum.tile([P, 4, P], F32, name="mm", tag="mm", bufs=3)
                for t in range(4):
                    c0 = 512 * g + 128 * t
                    for kp in range(2):
                        nc.tensor.matmul_mx(
                            out=ps[:, t, :],
                            lhsT=yq[:, kp, c0 : c0 + 128].bitcast(FP8X4),
                            lhsT_scale=ys[:, kp, c0 : c0 + 128],
                            rhs=xq[i][:, P * kp : P * kp + P].bitcast(FP8X4),
                            rhs_scale=xqs[i][:, P * kp : P * kp + P],
                            start=(kp == 0),
                            stop=(kp == 1),
                        )
                vps[i, g] = ps

        def v_out(i, gs=(0, 1)):
            if i not in vi:
                vi[i] = work.tile([P, 2, P, 4], BF16, name="vi", tag="vi", bufs=4, align_bytes=64)
            for g in gs:
                nc.scalar.copy(out=vi[i][:, g], in_=vps[i, g][:].rearrange("p t m -> p m t"))

        def v_quant(i):
            vq[i] = work.tile([P, 2 * P], U32, name="vq", tag="vq", bufs=3, align_bytes=64)
            vqs[i] = work.tile([P, 2 * P], U8, name="vqs", tag="vqs", bufs=3, align_bytes=64)
            parts = [(0, 1), (1, 2)] if i == TILES - 1 else [(0, 2)]
            for g0, g1 in parts:
                nc.vector.quantize_mx(
                    out=vq[i][:, P * g0 : P * g1].bitcast(FP8X4),
                    scales=vqs[i][:, P * g0 : P * g1],
                    in_=vi[i][:, g0:g1].rearrange("p g m t -> p (g m t)"),
                )

        ops = {}

        def o_mm(i, hs=(0, 1)):
            for h in hs:
                ps = psum.tile([P, 512], F32, name="ops", tag="ops", bufs=3)
                for g in range(2):
                    nc.tensor.matmul_mx(
                        out=ps[:],
                        lhsT=vq[i][:, P * g : P * g + P].bitcast(FP8X4),
                        lhsT_scale=vqs[i][:, P * g : P * g + P],
                        rhs=cq[:, g, 512 * h : 512 * h + 512].bitcast(FP8X4),
                        rhs_scale=cs[:, g, 512 * h : 512 * h + 512],
                        start=(g == 0),
                        stop=(g == 1),
                    )
                ops[i, h] = ps

        out_view = out.rearrange("(i p) n -> i p n", p=P)

        ot = {}

        def o_out(i, hs=(0, 1)):
            if i not in ot:
                ot[i] = work.tile([P, N], F32, name="ot", tag="ot", bufs=4, align_bytes=64)
            width = 256 if i == TILES - 1 else 512
            for h in hs:
                for c0 in range(0, 512, width):
                    c = slice(512 * h + c0, 512 * h + c0 + width)
                    nc.vector.tensor_tensor(out=ot[i][:, c], in0=ops[i, h][:, c0 : c0 + width], in1=gain_bc[:, c], op=MULT)
                    if i == TILES - 1:
                        nc.sync.dma_start(out=out_view[i][:, c], in_=ot[i][:, c])
                if h == 1 and i < TILES - 1:
                    nc.sync.dma_start(out=out_view[i], in_=ot[i][:])

        V, S = nc.vector.tensor_copy, nc.scalar.copy
        widen(1)
        widen(0)
        y_lay(0, 0, 3, S)
        y_lay(0, 0, 1, V)
        z_lay(0)
        turn(1)
        y_lay(0, 0, 0, S)
        turn(0)
        y_lay(1, 0, 0, V)
        y_lay(1, 0, 1, V)
        y_lay(0, 0, 2, V)
        y_lay(1, 0, 3, S)
        y_quant(1, 0, 0, 1)
        y_quant(0, 0, 0, 1)
        x_out(1)
        y_quant(1, 0, 1, 1)
        zy(0, 0, 0)
        y_lay(1, 0, 2, S)
        y_quant(0, 0, 1, 1)
        x_out(0)
        z_lay(1)
        y_quant(1, 0, 2, 2)
        zy(0, 1, 0)
        y_lay(0, 1, 0, V)
        d_out(0, 0, 0)
        zy(0, 1, 1)
        x_quant(0)
        c_out(0, 0, 0, "S")
        d_out(0, 1, 0)
        c_out(0, 1, 0, "S")
        zy(0, 0, 1)
        y_lay(1, 1, 1, V)
        c_out(0, 1, 1, "S")
        y_quant(0, 0, 2, 2)
        y_lay(0, 1, 3, V)
        x_quant(1)
        zy(0, 3, 0)
        y_lay(1, 1, 3, S)
        c_out(0, 0, 1, "S")
        zy(0, 2, 1)
        y_lay(0, 1, 2, V)
        widen(2)
        d_out(0, 3, 0)
        c_out(0, 3, 0, "S")
        y_lay(0, 1, 1, V)
        c_out(0, 2, 1, "S")
        y_lay(1, 1, 0, V)
        zy(0, 2, 0)
        y_lay(1, 1, 2, V)
        d_out(0, 2, 0)
        v_mm(0, (0,))
        y_quant(0, 1, 0, 4)
        c_out(0, 2, 0, "S")
        v_mm(1, (0,))
        v_out(0, (0,))
        v_out(1, (0,))
        zy(0, 3, 1)
        y_quant(1, 1, 0, 4)
        x_perm(2)
        zy(1, 3, 0)
        c_out(1, 3, 0, "S")
        c_out(0, 3, 1, "V")
        zy(1, 0, 1)
        d_add(0, 1, 0)
        d_add(0, 0, 0)
        d_out(1, 0, 1)
        widen(3)
        c_out(1, 0, 1, "S")
        c_quant(1, 0)
        v_mm(0, (1,))
        d_add(0, 2, 0)
        v_out(0, (1,))
        zy(1, 1, 0)
        x_perm(3)
        zy(1, 0, 0)
        zy(1, 2, 0)
        c_out(1, 1, 0, "V")
        turn(2)
        d_add(0, 3, 0)
        c_out(1, 0, 0, "S")
        turn(3)
        c_out(1, 2, 0, "S")
        v_mm(1, (1,))
        v_quant(0)
        c_quant(0, 0)
        widen(4)
        c_quant(0, 1)
        x_out(2)
        zy(1, 2, 1)
        v_out(1, (1,))
        zy(1, 1, 1)
        widen(5)
        d_out(1, 2, 1)
        v_quant(1)
        zy(1, 3, 1)
        x_quant(2)
        x_out(3)
        o_mm(0, (0,))
        c_out(1, 2, 1, "S")
        o_mm(1, (0,))
        d_out(1, 1, 1)
        d_add(1, 2, 1)
        c_out(1, 1, 1, "V")
        d_out(1, 3, 1)
        v_mm(2, (1,))
        c_out(1, 3, 1, "S")
        v_mm(2, (0,))
        o_out(0, (0,))
        d_add(1, 0, 1)
        o_out(1, (0,))
        d_add(1, 1, 1)
        d_add(1, 3, 1)
        x_perm(5)
        x_perm(4)
        v_out(2, (0,))
        x_quant(3)
        c_quant(1, 1)
        turn(5)
        turn(4)
        widen(6)
        v_out(2, (1,))
        x_out(5)
        x_out(4)
        o_mm(1, (1,))
        v_quant(2)
        o_out(1, (1,))
        o_mm(0, (1,))
        x_perm(6)
        x_quant(5)
        o_out(0, (1,))
        x_quant(4)
        v_mm(3, (0,))
        v_mm(3, (1,))
        v_out(3, (0,))
        v_out(3, (1,))
        widen(7)
        o_mm(2, (0,))
        o_mm(2, (1,))
        v_quant(3)
        x_perm(7)
        o_out(2, (0,))
        o_out(2, (1,))
        v_mm(4, (0,))
        v_mm(4, (1,))
        v_out(4, (0,))
        v_out(4, (1,))
        widen(8)
        o_mm(3, (0,))
        o_mm(3, (1,))
        v_quant(4)
        o_out(3, (0,))
        o_out(3, (1,))
        turn(6)
        turn(7)
        x_out(6)
        x_out(7)
        x_perm(8)
        x_quant(6)
        x_quant(7)
        v_mm(5, (0,))
        v_mm(5, (1,))
        v_out(5, (0,))
        v_out(5, (1,))
        widen(9)
        o_mm(4, (0,))
        o_mm(4, (1,))
        v_quant(5)
        x_perm(9)
        o_out(4, (0,))
        o_out(4, (1,))
        v_mm(6, (0,))
        v_mm(6, (1,))
        v_out(6, (0,))
        v_out(6, (1,))
        widen(10)
        o_mm(5, (0,))
        o_mm(5, (1,))
        v_quant(6)
        o_out(5, (0,))
        o_out(5, (1,))
        turn(8)
        turn(9)
        x_out(8)
        x_out(9)
        x_perm(10)
        x_quant(8)
        x_quant(9)
        v_mm(7, (0,))
        v_mm(7, (1,))
        v_out(7, (0,))
        v_out(7, (1,))
        widen(11)
        o_mm(6, (0,))
        o_mm(6, (1,))
        v_quant(7)
        x_perm(11)
        o_out(6, (0,))
        o_out(6, (1,))
        v_mm(8, (0,))
        v_mm(8, (1,))
        v_out(8, (0,))
        v_out(8, (1,))
        o_mm(7, (0,))
        o_mm(7, (1,))
        v_quant(8)
        o_out(7, (0,))
        o_out(7, (1,))
        turn(10)
        turn(11)
        x_out(10)
        x_out(11)
        x_quant(10)
        x_quant(11)
        v_mm(9, (0,))
        v_mm(9, (1,))
        v_out(9, (0,))
        v_out(9, (1,))
        o_mm(8, (0,))
        o_mm(8, (1,))
        v_quant(9)
        o_out(8, (0,))
        o_out(8, (1,))
        v_mm(10, (0,))
        v_mm(10, (1,))
        v_out(10, (0,))
        v_out(10, (1,))
        o_mm(9, (0,))
        o_mm(9, (1,))
        v_quant(10)
        o_out(9, (0,))
        o_out(9, (1,))
        v_mm(11, (0,))
        v_mm(11, (1,))
        v_out(11, (0,))
        v_out(11, (1,))
        o_mm(10, (0,))
        o_mm(10, (1,))
        v_quant(11)
        o_out(10, (0,))
        o_out(10, (1,))
        o_mm(11, (0,))
        o_mm(11, (1,))
        o_out(11, (0,))
        o_out(11, (1,))
